import numpy as np
import ml_dtypes


def mxq(x, axis, fmt="e4m3"):
    dtype, down = {"e4m3": (ml_dtypes.float8_e4m3fn, 7), "e5m2": (ml_dtypes.float8_e5m2, 14)}[fmt]
    v = np.moveaxis(np.asarray(x, np.float32).astype(ml_dtypes.bfloat16).astype(np.float64), axis, -1)
    blocks = v.reshape(v.shape[:-1] + (-1, 32))
    amax = np.abs(blocks).max(-1, keepdims=True)
    byte = np.maximum(np.where(amax > 0, np.frexp(amax)[1] - 1 + 127, 0) - down, 1)
    scale = np.exp2(byte - 127.0)
    codes = (blocks / scale).astype(np.float32).astype(dtype).astype(np.float64)
    return np.moveaxis((codes * scale).reshape(v.shape), -1, axis)


WIDE = False


def mx_kscale(k):
    if not WIDE:
        return np.ones(k)
    levels = np.array([10, -10, 5, -5, 0])
    if k % 512:
        return np.exp2(np.random.permutation(np.resize(levels, k // 32))).repeat(32)
    a = np.empty((k // 512, 16))
    for p in range(k // 512):
        a[p, :8] = np.random.permutation(np.resize(levels, 8))
        for g in range(8):
            far = levels[np.abs(levels - a[p, g]) >= 10]
            a[p, g + 8] = far[np.random.randint(len(far))]
    return np.exp2(a.ravel()).repeat(32)


def f64(x):
    return np.asarray(x).astype(np.float64)


def striped(idx):
    return np.tile(np.asarray(idx).reshape(-1, 16).T, (8, 1)).astype(np.uint16)


def unstriped(offs):
    return offs[:16].T.reshape(-1).astype(np.int64)


E2M1 = np.array([0.0, 0.5, 1.0, 1.5, 2.0, 3.0, 4.0, 6.0, -0.0, -0.5, -1.0, -1.5, -2.0, -3.0, -4.0, -6.0])


def pack_weight(w, fmt):
    k, n = w.shape
    w = f64(np.asarray(w, np.float32).astype(ml_dtypes.bfloat16)).reshape(k // 32, 32, n)
    amax = np.abs(w).max(1)
    if fmt == "e4m3":
        byte = np.frexp(amax)[1] - 1 + 127 - 7
    else:
        mant, ex = np.frexp(amax / 6.0)
        byte = np.where(mant > 0.5, ex, ex - 1) + 127
    byte = np.clip(np.where(amax > 0, byte, 1), 1, 254)
    scaled = (w * np.exp2(127.0 - byte)[:, None, :]).reshape(k, n).astype(np.float32)
    by_word = np.ascontiguousarray(scaled.reshape(k // 512, 128, 4, n).transpose(0, 1, 3, 2))
    if fmt == "e4m3":
        words = by_word.astype(ml_dtypes.float8_e4m3fn).view(np.uint8)
    else:
        c = by_word.astype(ml_dtypes.float4_e2m1fn).view(np.uint8) & 0xF
        words = (c[..., 0::2] | (c[..., 1::2] << 4)).reshape(k // 512, 128, 2 * n)
    return np.ascontiguousarray(words), np.ascontiguousarray(byte.astype(np.uint8).reshape(k // 512, 16, n))


def unpack_weight(words, scales, fmt):
    g, _, n = scales.shape
    words = np.ascontiguousarray(words).reshape(g, 128, n, -1)
    if fmt == "e4m3":
        vals = words.view(ml_dtypes.float8_e4m3fn).astype(np.float64)
    else:
        nib = np.empty((g, 128, n, 4), np.uint8)
        nib[..., 0::2] = words & 0xF
        nib[..., 1::2] = words >> 4
        vals = E2M1[nib]
    vals = vals * np.repeat(np.exp2(scales.astype(np.float64) - 127.0), 8, axis=1)[..., None]
    return vals.transpose(0, 1, 3, 2).reshape(g * 512, n)


K, T, J, I, N, R = 1024, 1024, 512, 512, 512, 512


def setup_inputs():
    n = np.random.standard_normal
    idx = np.random.permutation(T)[:J]
    idx2 = np.random.permutation(T)[:I]
    fk = mx_kscale(K)
    fr = mx_kscale(R)
    xqp = pack_weight(n((K, T)) / fk[:, None], "e4m3")
    wap = pack_weight(n((K, N)) * 1 / np.sqrt(K) * fk[:, None], "e2m1")
    lowp = pack_weight(n((K, R)) * 1 / np.sqrt(K) * fk[:, None] * fr, "e4m3")
    upp = pack_weight(n((R, N)) * 1 / np.sqrt(R) / fr[:, None], "e2m1")
    return {
        "xq_words": xqp[0],
        "xq_scales": xqp[1],
        "wa_words": wap[0],
        "wa_scales": wap[1],
        "low_words": lowp[0],
        "low_scales": lowp[1],
        "up_words": upp[0],
        "up_scales": upp[1],
        "ga": (np.random.uniform(0.4, 1.2, (1, J))).astype(np.float32),
        "offs": striped(idx),
        "offs2": striped(idx2),
    }


def reference(xq_words, xq_scales, wa_words, wa_scales, low_words, low_scales, up_words, up_scales, ga, offs, offs2):
    idx = unstriped(offs)
    idx2 = unstriped(offs2)
    xqu = unpack_weight(xq_words, xq_scales, "e4m3")
    wau = unpack_weight(wa_words, wa_scales, "e2m1")
    lowu = unpack_weight(low_words, low_scales, "e4m3")
    upu = unpack_weight(up_words, up_scales, "e2m1")
    xqidxg = xqu[:, idx]
    p = wau.T @ xqidxg
    xqidx2g = xqu[:, idx2]
    u = lowu.T @ xqidx2g
    v = np.abs(u) - 0.5 * u
    vq = mxq(v, 0, "e4m3")
    q = upu.T @ vq
    pw = p * f64(ga)
    pg = np.zeros((N, T))
    pg[:, idx] = pw
    qg = np.zeros((N, T))
    qg[:, idx2] = q
    y = pg + qg
    return y

@@ -1,0 +1,229 @@
+from contextlib import ExitStack
+
+import concourse.mybir as mybir
+from concourse.masks import make_identity
+
+K, T, J, N, R = 1024, 1024, 512, 512, 512
+FLOPS = 2 * K * N * J + 2 * K * R * J + 2 * R * N * J
+
+F32 = mybir.dt.float32
+BF16 = mybir.dt.bfloat16
+I32 = mybir.dt.int32
+U32 = mybir.dt.uint32
+U16 = mybir.dt.uint16
+U8 = mybir.dt.uint8
+FP8X4 = mybir.dt.float8_e4m3fn_x4
+FP4X4 = mybir.dt.float4_e2m1fn_x4
+ACT = mybir.ActivationFunctionType
+ALU = mybir.AluOpType
+
+P = 128
+PASSES = K // 512
+TILES = 4
+BANK = 512
+
+
+def tile_list_two_roads_one_layer_kernel(
+    tc, xq_words, xq_scales, wa_words, wa_scales, low_words, low_scales, up_words, up_scales, ga, offs, offs2, out
+):
+    nc = tc.nc
+    with ExitStack() as ctx:
+        lists = ctx.enter_context(tc.tile_pool(name="lists", bufs=1))
+        sb = ctx.enter_context(tc.tile_pool(name="sb", bufs=1))
+        psum = ctx.enter_context(tc.psum_pool(name="psum", bufs=1))
+
+        def sbuf(shape, dtype, name, tag=None):
+            return sb.tile(shape, dtype, name=name, tag=tag or name, align_bytes=64)
+
+        def bank(b, name):
+            return psum.tile([P, BANK], F32, name=name, tag="bank%d" % b)
+
+        list1 = lists.tile([P, J // 16], U16, name="list1")
+        list2 = lists.tile([P, J // 16], U16, name="list2")
+
+        xq_s = sbuf([P, T], U8, "xq_s")
+        wa_s = sbuf([P, PASSES * N], U8, "wa_s")
+        low_s = sbuf([P, R], U8, "low_s")
+        up_s = sbuf([P, N], U8, "up_s")
+        x1_s_hi = sbuf([P, J], U8, "x1_s_hi")
+        for plane in (xq_s, wa_s, x1_s_hi, low_s, up_s):
+            nc.vector.memset(plane[:].bitcast(I32), 0)
+
+        xq_w = [sbuf([P, T], I32, "xq_w%d" % z, tag="late_page%d" % z) for z in range(PASSES)]
+        wa_w = sbuf([P, PASSES * 2 * N], U8, "wa_w")
+        low_w = sbuf([P, PASSES * R], I32, "low_w", tag="late_page2")
+        up_w = sbuf([P, 2 * N], U8, "up_w")
+        ga_col = sbuf([P, 4], F32, "ga_col")
+
+        nc.sync.dma_start(list1[:], offs)
+        for q in range(4):
+            nc.scalar.dma_start(
+                xq_s[32 * q : 32 * q + 8, :].bitcast(I32), xq_scales[:, 4 * q : 4 * q + 4, :].bitcast(I32)
+            )
+        for z in range(PASSES):
+            nc.sync.dma_start(xq_w[z][:], xq_words[z].rearrange("p t i -> p (t i)").bitcast(I32))
+        nc.sync.dma_start(list2[:], offs2)
+        nc.sync.dma_start(
+            wa_w[:].bitcast(I32).rearrange("p (z c) -> p z c", z=PASSES),
+            wa_words.bitcast(I32).rearrange("z p c -> p z c"),
+        )
+        for q in range(4):
+            nc.scalar.dma_start(
+                wa_s[32 * q : 32 * q + 4, :].bitcast(I32).rearrange("p (z c) -> p z c", z=PASSES),
+                wa_scales[:, 4 * q : 4 * q + 4, :].bitcast(I32).rearrange("z r c -> r z c"),
+            )
+        nc.sync.dma_start(ga_col[:], ga.rearrange("o (p m) -> (o p) m", m=4))
+        nc.sync.dma_start(
+            low_w[:].rearrange("p (z c) -> p z c", z=PASSES),
+            low_words.rearrange("z p r i -> p z (r i)").bitcast(I32),
+        )
+        for q in range(4):
+            nc.scalar.dma_start(
+                low_s[32 * q : 32 * q + 8, :].bitcast(I32), low_scales[:, 4 * q : 4 * q + 4, :].bitcast(I32)
+            )
+
+        ident = sbuf([P, P], F32, "ident")
+        make_identity(nc, ident[:])
+
+        page1 = [sbuf([P, T], F32, "page1_%d" % c) for c in range(TILES - 1)]
+        for page in page1:
+            nc.vector.memset(page[:], 0.0)
+
+        x1_s = sbuf([P, J], U8, "x1_s")
+        x2_s = sbuf([P, J], U8, "x2_s")
+        x1_w = [sbuf([P, J], U32, "x1_w%d" % z) for z in range(PASSES)]
+        x2_w = [sbuf([P, J], U32, "x2_w%d" % z) for z in range(PASSES)]
+        nc.vector.tensor_copy(x1_s[:], xq_s[:].indirect(list1[:]))
+        nc.sync.dma_start(x1_s_hi[0:112, :].bitcast(I32), x1_s[4:116, :].bitcast(I32))
+        for z in range(PASSES):
+            nc.vector.tensor_copy(x1_w[z][:], xq_w[z][:].bitcast(U32).indirect(list1[:]))
+        nc.vector.tensor_copy(x2_s[:], xq_s[:].indirect(list2[:]))
+        for z in range(PASSES):
+            nc.vector.tensor_copy(x2_w[z][:], xq_w[z][:].bitcast(U32).indirect(list2[:]))
+
+        nc.sync.dma_start(up_w[:].bitcast(I32), up_words[0].bitcast(I32))
+        for q in range(4):
+            nc.sync.dma_start(
+                up_s[32 * q : 32 * q + 4, :].bitcast(I32), up_scales[0, 4 * q : 4 * q + 4, :].bitcast(I32)
+            )
+
+        ga_bank = bank(0, "ga_bank")
+        for m in range(4):
+            nc.tensor.transpose(ga_bank[:, P * m : P * (m + 1)], ga_col[:, m : m + 1].to_broadcast([P, P]), ident[:])
+        ga_all = sbuf([P, J], F32, "ga_all")
+        nc.scalar.activation(
+            ga_all[:].rearrange("p (j m) -> p j m", m=4), ga_bank[:].rearrange("p (m j) -> p j m", m=4), ACT.Copy
+        )
+
+        x1_planes = (x1_s, x1_s_hi)
+
+        def first_road(c, tag):
+            acc = bank(4 + c, "p_bank%d" % c)
+            for z in range(PASSES):
+                nc.tensor.matmul_mx(
+                    out=acc[:],
+                    lhsT=wa_w[:, 2 * (N * z + P * c) : 2 * (N * z + P * (c + 1))].bitcast(FP4X4),
+                    lhsT_scale=wa_s[:, N * z + P * c : N * z + P * (c + 1)],
+                    rhs=x1_w[z][:].bitcast(FP8X4),
+                    rhs_scale=x1_planes[z][:],
+                    start=(z == 0),
+                    stop=(z == PASSES - 1),
+                )
+            p_sb = sbuf([P, J], F32, "p_sb%d" % c, tag=tag)
+            nc.scalar.copy(p_sb[:], acc[:])
+            return p_sb
+
+        def place_first(c, p_sb):
+            nc.vector.tensor_tensor(page1[c][:].indirect(list1[:]), p_sb[:], ga_all[:], ALU.mult)
+
+        for c in range(TILES - 1):
+            place_first(c, first_road(c, None))
+
+        u_banks = [bank(2 + c, "u_bank%d" % c) for c in range(TILES)]
+        for z in range(PASSES):
+            for c in range(TILES):
+                nc.tensor.matmul_mx(
+                    out=u_banks[c][:],
+                    lhsT=x2_w[z][:, P * c : P * (c + 1)].bitcast(FP8X4),
+                    lhsT_scale=x2_s[4 * z : P, P * c : P * (c + 1)],
+                    rhs=low_w[:, R * z : R * (z + 1)].bitcast(FP8X4),
+                    rhs_scale=low_s[4 * z : P, :],
+                    start=(z == 0),
+                    stop=(z == PASSES - 1),
+                )
+
+        page2 = [sbuf([P, T], F32, "page2_%d" % z, tag="late_page%d" % z) for z in range(2)]
+        page1.append(sbuf([P, T], F32, "page1_3", tag="late_page2"))
+        for page in (page1[3], page2[0], page2[1]):
+            nc.gpsimd.memset(page[:], 0.0)
+
+        v_bf = sbuf([P, 4 * J], BF16, "v_bf")
+        for c in range(TILES):
+            u_dealt = u_banks[c][:].rearrange("p (q t) -> p t q", t=4)
+            terms = [sbuf([P, R], F32, "u_abs%d" % c), sbuf([P, R], F32, "u_half%d" % c)]
+            nc.scalar.activation(terms[0][:].rearrange("p (t q) -> p t q", t=4), u_dealt, ACT.Abs)
+            nc.scalar.activation(terms[1][:].rearrange("p (t q) -> p t q", t=4), u_dealt, ACT.Copy, scale=-0.5)
+            v_bank = bank(c % 2, "v_bank%d" % c)
+            for s in range(2):
+                for t in range(4):
+                    nc.tensor.matmul(
+                        v_bank[:, P * t : P * (t + 1)],
+                        lhsT=terms[s][:, P * t : P * (t + 1)],
+                        rhs=ident[:],
+                        is_transpose=True,
+                        start=(s == 0 and t == 0),
+                        stop=(s == 1 and t == 3),
+                    )
+            nc.scalar.copy(
+                v_bf[:, 4 * P * c : 4 * P * (c + 1)].rearrange("p (i t) -> p i t", t=4),
+                v_bank[:].rearrange("p (t i) -> p i t", t=4),
+            )
+
+        v_w = sbuf([P, J], U32, "v_w")
+        v_s = sbuf([P, J], U8, "v_s")
+        nc.vector.quantize_mx(out=v_w[:].bitcast(FP8X4), scales=v_s[:], in_=v_bf[:])
+
+        place_first(TILES - 1, first_road(TILES - 1, "u_half%d" % (TILES - 1)))
+
+        q_sb = []
+        for c in range(TILES):
+            acc = bank((6, 4, 5, 7)[c], "q_bank%d" % c)
+            nc.tensor.matmul_mx(
+                out=acc[:],
+                lhsT=up_w[:, 2 * P * c : 2 * P * (c + 1)].bitcast(FP4X4),
+                lhsT_scale=up_s[:, P * c : P * (c + 1)],
+                rhs=v_w[:].bitcast(FP8X4),
+                rhs_scale=v_s[:],
+                start=True,
+                stop=True,
+            )
+            q_sb.append(sbuf([P, J], F32, "q_sb%d" % c))
+            nc.scalar.copy(q_sb[c][:], acc[:])
+
+        for c in range(TILES):
+            pages = (page1[c], page2[c % 2])
+            nc.vector.tensor_copy(pages[1][:].indirect(list2[:]), q_sb[c][:])
+            for h in range(2):
+                cols = slice(BANK * h, BANK * (h + 1))
+                y = sbuf([P, BANK], F32, "y%d_%d" % (c, h))
+                if c == TILES - 1:
+                    nc.vector.tensor_tensor(y[:], pages[0][:, cols], pages[1][:, cols], ALU.add)
+                else:
+                    sum_bank = bank(h, "sum_bank%d_%d" % (c, h))
+                    for s in range(2):
+                        for j in range(4):
+                            nc.tensor.matmul(
+                                sum_bank[:, P * j : P * (j + 1)],
+                                lhsT=pages[s][:, BANK * h + P * j : BANK * h + P * (j + 1)],
+                                rhs=ident[:],
+                                is_transpose=True,
+                                start=(s == 0 and j == 0),
+                                stop=(s == 1 and j == 3),
+                            )
+                    y_t = sbuf([P, BANK], F32, "y_t%d_%d" % (c, h))
+                    nc.scalar.copy(y_t[:], sum_bank[:])
+                    back_bank = bank(2 + h, "back_bank%d_%d" % (c, h))
+                    for j in range(4):
+                        nc.tensor.transpose(back_bank[:, P * j : P * (j + 1)], y_t[:, P * j : P * (j + 1)], ident[:])
+                    nc.scalar.copy(y[:], back_bank[:])
+                nc.sync.dma_start(out[P * c : P * (c + 1), cols], y[:])

@@ -21,6 +21,7 @@ P = 128
 PASSES = K // 512
 TILES = 4
 BANK = 512
+SPLIT = 288
 
 
 def tile_list_two_roads_one_layer_kernel(
@@ -46,48 +47,55 @@ def tile_list_two_roads_one_layer_kernel(
         low_s = sbuf([P, R], U8, "low_s")
         up_s = sbuf([P, N], U8, "up_s")
         x1_s_hi = sbuf([P, J], U8, "x1_s_hi")
-        for plane in (xq_s, wa_s, x1_s_hi, low_s, up_s):
+        for plane in (xq_s, low_s):
+            nc.gpsimd.memset(plane[:].bitcast(I32), 0)
+        for plane in (wa_s, x1_s_hi):
             nc.vector.memset(plane[:].bitcast(I32), 0)
 
-        xq_w = [sbuf([P, T], I32, "xq_w%d" % z, tag="late_page%d" % z) for z in range(PASSES)]
+        xq_w = sbuf([P, PASSES * T], I32, "xq_w")
         wa_w = sbuf([P, PASSES * 2 * N], U8, "wa_w")
-        low_w = sbuf([P, PASSES * R], I32, "low_w", tag="late_page2")
-        up_w = sbuf([P, 2 * N], U8, "up_w")
+        low_w = sbuf([P, PASSES * R], I32, "low_w")
         ga_col = sbuf([P, 4], F32, "ga_col")
 
         nc.sync.dma_start(list1[:], offs)
+        nc.sync.dma_start(list2[:], offs2)
         for q in range(4):
-            nc.scalar.dma_start(
+            nc.sync.dma_start(
                 xq_s[32 * q : 32 * q + 8, :].bitcast(I32), xq_scales[:, 4 * q : 4 * q + 4, :].bitcast(I32)
             )
-        for z in range(PASSES):
-            nc.sync.dma_start(xq_w[z][:], xq_words[z].rearrange("p t i -> p (t i)").bitcast(I32))
-        nc.sync.dma_start(list2[:], offs2)
+        nc.sync.dma_start(
+            xq_w[:].rearrange("p (z t) -> p z t", z=PASSES),
+            xq_words.rearrange("z p t i -> p z (t i)").bitcast(I32),
+        )
         nc.sync.dma_start(
             wa_w[:].bitcast(I32).rearrange("p (z c) -> p z c", z=PASSES),
             wa_words.bitcast(I32).rearrange("z p c -> p z c"),
         )
         for q in range(4):
-            nc.scalar.dma_start(
+            nc.sync.dma_start(
                 wa_s[32 * q : 32 * q + 4, :].bitcast(I32).rearrange("p (z c) -> p z c", z=PASSES),
                 wa_scales[:, 4 * q : 4 * q + 4, :].bitcast(I32).rearrange("z r c -> r z c"),
             )
-        nc.sync.dma_start(ga_col[:], ga.rearrange("o (p m) -> (o p) m", m=4))
+        nc.gpsimd.dma_start(ga_col[:], ga.rearrange("o (p m) -> (o p) m", m=4))
         nc.sync.dma_start(
             low_w[:].rearrange("p (z c) -> p z c", z=PASSES),
             low_words.rearrange("z p r i -> p z (r i)").bitcast(I32),
         )
+        ident = sbuf([P, P], F32, "ident")
+        make_identity(nc, ident[:])
         for q in range(4):
-            nc.scalar.dma_start(
+            nc.gpsimd.dma_start(
                 low_s[32 * q : 32 * q + 8, :].bitcast(I32), low_scales[:, 4 * q : 4 * q + 4, :].bitcast(I32)
             )
 
-        ident = sbuf([P, P], F32, "ident")
-        make_identity(nc, ident[:])
-
-        page1 = [sbuf([P, T], F32, "page1_%d" % c) for c in range(TILES - 1)]
-        for page in page1:
-            nc.vector.memset(page[:], 0.0)
+        page1 = [sbuf([P, T], F32, "page1_%d" % c) for c in range(TILES)]
+        page2 = [sbuf([P, T], F32, "page2_%d" % c) for c in range(TILES)]
+        nc.vector.memset(page1[0][:], 0.0)
+        for page in page1[1:]:
+            nc.gpsimd.memset(page[:], 0.0)
+        nc.gpsimd.memset(up_s[:].bitcast(I32), 0)
+        for page in page2:
+            nc.gpsimd.memset(page[:], 0.0)
 
         x1_s = sbuf([P, J], U8, "x1_s")
         x2_s = sbuf([P, J], U8, "x2_s")
@@ -95,12 +103,12 @@ def tile_list_two_roads_one_layer_kernel(
         x2_w = [sbuf([P, J], U32, "x2_w%d" % z) for z in range(PASSES)]
         nc.vector.tensor_copy(x1_s[:], xq_s[:].indirect(list1[:]))
         nc.sync.dma_start(x1_s_hi[0:112, :].bitcast(I32), x1_s[4:116, :].bitcast(I32))
-        for z in range(PASSES):
-            nc.vector.tensor_copy(x1_w[z][:], xq_w[z][:].bitcast(U32).indirect(list1[:]))
         nc.vector.tensor_copy(x2_s[:], xq_s[:].indirect(list2[:]))
-        for z in range(PASSES):
-            nc.vector.tensor_copy(x2_w[z][:], xq_w[z][:].bitcast(U32).indirect(list2[:]))
+        for x_w, entries in ((x1_w, list1), (x2_w, list2)):
+            for z in range(PASSES):
+                nc.vector.tensor_copy(x_w[z][:], xq_w[:, T * z : T * (z + 1)].bitcast(U32).indirect(entries[:]))
 
+        up_w = sbuf([P, 2 * N], U8, "up_w", tag="xq_s")
         nc.sync.dma_start(up_w[:].bitcast(I32), up_words[0].bitcast(I32))
         for q in range(4):
             nc.sync.dma_start(
@@ -117,7 +125,7 @@ def tile_list_two_roads_one_layer_kernel(
 
         x1_planes = (x1_s, x1_s_hi)
 
-        def first_road(c, tag):
+        def first_road(c):
             acc = bank(4 + c, "p_bank%d" % c)
             for z in range(PASSES):
                 nc.tensor.matmul_mx(
@@ -129,15 +137,17 @@ def tile_list_two_roads_one_layer_kernel(
                     start=(z == 0),
                     stop=(z == PASSES - 1),
                 )
-            p_sb = sbuf([P, J], F32, "p_sb%d" % c, tag=tag)
-            nc.scalar.copy(p_sb[:], acc[:])
-            return p_sb
+            return acc
 
-        def place_first(c, p_sb):
-            nc.vector.tensor_tensor(page1[c][:].indirect(list1[:]), p_sb[:], ga_all[:], ALU.mult)
+        def place_first(c, acc, j0, j1, tag):
+            p_sb = sbuf([P, J], F32, "p_sb%d_%d" % (c, j0), tag=tag)
+            nc.scalar.copy(p_sb[:, j0:j1], acc[:, j0:j1])
+            nc.vector.tensor_tensor(
+                page1[c][:].indirect(list1[:, j0 // 16 : j1 // 16]), p_sb[:, j0:j1], ga_all[:, j0:j1], ALU.mult
+            )
 
         for c in range(TILES - 1):
-            place_first(c, first_road(c, None))
+            place_first(c, first_road(c), 0, J, None)
 
         u_banks = [bank(2 + c, "u_bank%d" % c) for c in range(TILES)]
         for z in range(PASSES):
@@ -151,11 +161,6 @@ def tile_list_two_roads_one_layer_kernel(
                     start=(z == 0),
                     stop=(z == PASSES - 1),
                 )
-
-        page2 = [sbuf([P, T], F32, "page2_%d" % z, tag="late_page%d" % z) for z in range(2)]
-        page1.append(sbuf([P, T], F32, "page1_3", tag="late_page2"))
-        for page in (page1[3], page2[0], page2[1]):
-            nc.gpsimd.memset(page[:], 0.0)
 
         v_bf = sbuf([P, 4 * J], BF16, "v_bf")
         for c in range(TILES):
@@ -183,11 +188,12 @@ def tile_list_two_roads_one_layer_kernel(
         v_s = sbuf([P, J], U8, "v_s")
         nc.vector.quantize_mx(out=v_w[:].bitcast(FP8X4), scales=v_s[:], in_=v_bf[:])
 
-        place_first(TILES - 1, first_road(TILES - 1, "u_half%d" % (TILES - 1)))
+        p_last = first_road(TILES - 1)
+        place_first(TILES - 1, p_last, 0, SPLIT, "u_half%d" % (TILES - 1))
 
         q_sb = []
         for c in range(TILES):
-            acc = bank((6, 4, 5, 7)[c], "q_bank%d" % c)
+            acc = bank((6, 4, 5, 2)[c], "q_bank%d" % c)
             nc.tensor.matmul_mx(
                 out=acc[:],
                 lhsT=up_w[:, 2 * P * c : 2 * P * (c + 1)].bitcast(FP4X4),
@@ -201,29 +207,36 @@ def tile_list_two_roads_one_layer_kernel(
             nc.scalar.copy(q_sb[c][:], acc[:])
 
         for c in range(TILES):
-            pages = (page1[c], page2[c % 2])
-            nc.vector.tensor_copy(pages[1][:].indirect(list2[:]), q_sb[c][:])
+            nc.vector.tensor_copy(page2[c][:].indirect(list2[:]), q_sb[c][:])
+
+        for c in range(TILES - 1):
+            if c == TILES - 2:
+                place_first(TILES - 1, p_last, SPLIT, J, "y_t%d_1" % (c - 1))
+            pages = (page1[c], page2[c])
             for h in range(2):
                 cols = slice(BANK * h, BANK * (h + 1))
                 y = sbuf([P, BANK], F32, "y%d_%d" % (c, h))
-                if c == TILES - 1:
-                    nc.vector.tensor_tensor(y[:], pages[0][:, cols], pages[1][:, cols], ALU.add)
-                else:
-                    sum_bank = bank(h, "sum_bank%d_%d" % (c, h))
-                    for s in range(2):
-                        for j in range(4):
-                            nc.tensor.matmul(
-                                sum_bank[:, P * j : P * (j + 1)],
-                                lhsT=pages[s][:, BANK * h + P * j : BANK * h + P * (j + 1)],
-                                rhs=ident[:],
-                                is_transpose=True,
-                                start=(s == 0 and j == 0),
-                                stop=(s == 1 and j == 3),
-                            )
-                    y_t = sbuf([P, BANK], F32, "y_t%d_%d" % (c, h))
-                    nc.scalar.copy(y_t[:], sum_bank[:])
-                    back_bank = bank(2 + h, "back_bank%d_%d" % (c, h))
+                sum_bank = bank(h, "sum_bank%d_%d" % (c, h))
+                for s in range(2):
                     for j in range(4):
-                        nc.tensor.transpose(back_bank[:, P * j : P * (j + 1)], y_t[:, P * j : P * (j + 1)], ident[:])
-                    nc.scalar.copy(y[:], back_bank[:])
-                nc.sync.dma_start(out[P * c : P * (c + 1), cols], y[:])
+                        nc.tensor.matmul(
+                            sum_bank[:, P * j : P * (j + 1)],
+                            lhsT=pages[s][:, BANK * h + P * j : BANK * h + P * (j + 1)],
+                            rhs=ident[:],
+                            is_transpose=True,
+                            start=(s == 0 and j == 0),
+                            stop=(s == 1 and j == 3),
+                        )
+                y_t = sbuf([P, BANK], F32, "y_t%d_%d" % (c, h))
+                nc.scalar.copy(y_t[:], sum_bank[:])
+                back_bank = bank(2 + h, "back_bank%d_%d" % (c, h))
+                for j in range(4):
+                    nc.tensor.transpose(back_bank[:, P * j : P * (j + 1)], y_t[:, P * j : P * (j + 1)], ident[:])
+                nc.scalar.copy(y[:], back_bank[:])
+                nc.scalar.dma_start(out[P * c : P * (c + 1), cols], y[:])
+
+        c = TILES - 1
+        for t0, t1, queue in ((0, 512, nc.sync), (512, 768, nc.sync), (768, 1024, nc.sync)):
+            y = sbuf([P, t1 - t0], F32, "y_last%d" % t0)
+            nc.vector.tensor_tensor(y[:], page1[c][:, t0:t1], page2[c][:, t0:t1], ALU.add)
+            queue.dma_start(out[P * c : P * (c + 1), t0:t1], y[:])

@@ -21,7 +21,7 @@ P = 128
 PASSES = K // 512
 TILES = 4
 BANK = 512
-SPLIT = 288
+SPLIT = 320
 
 
 def tile_list_two_roads_one_layer_kernel(
@@ -45,16 +45,13 @@ def tile_list_two_roads_one_layer_kernel(
         xq_s = sbuf([P, T], U8, "xq_s")
         wa_s = sbuf([P, PASSES * N], U8, "wa_s")
         low_s = sbuf([P, R], U8, "low_s")
-        up_s = sbuf([P, N], U8, "up_s")
         x1_s_hi = sbuf([P, J], U8, "x1_s_hi")
-        for plane in (xq_s, low_s):
-            nc.gpsimd.memset(plane[:].bitcast(I32), 0)
+        nc.gpsimd.memset(xq_s[:].bitcast(I32), 0)
         for plane in (wa_s, x1_s_hi):
             nc.vector.memset(plane[:].bitcast(I32), 0)
 
         xq_w = sbuf([P, PASSES * T], I32, "xq_w")
         wa_w = sbuf([P, PASSES * 2 * N], U8, "wa_w")
-        low_w = sbuf([P, PASSES * R], I32, "low_w")
         ga_col = sbuf([P, 4], F32, "ga_col")
 
         nc.sync.dma_start(list1[:], offs)
@@ -76,26 +73,14 @@ def tile_list_two_roads_one_layer_kernel(
                 wa_s[32 * q : 32 * q + 4, :].bitcast(I32).rearrange("p (z c) -> p z c", z=PASSES),
                 wa_scales[:, 4 * q : 4 * q + 4, :].bitcast(I32).rearrange("z r c -> r z c"),
             )
-        nc.gpsimd.dma_start(ga_col[:], ga.rearrange("o (p m) -> (o p) m", m=4))
-        nc.sync.dma_start(
-            low_w[:].rearrange("p (z c) -> p z c", z=PASSES),
-            low_words.rearrange("z p r i -> p z (r i)").bitcast(I32),
-        )
+        nc.sync.dma_start(ga_col[:], ga.rearrange("o (p m) -> (o p) m", m=4))
         ident = sbuf([P, P], F32, "ident")
         make_identity(nc, ident[:])
-        for q in range(4):
-            nc.gpsimd.dma_start(
-                low_s[32 * q : 32 * q + 8, :].bitcast(I32), low_scales[:, 4 * q : 4 * q + 4, :].bitcast(I32)
-            )
 
-        page1 = [sbuf([P, T], F32, "page1_%d" % c) for c in range(TILES)]
-        page2 = [sbuf([P, T], F32, "page2_%d" % c) for c in range(TILES)]
-        nc.vector.memset(page1[0][:], 0.0)
-        for page in page1[1:]:
-            nc.gpsimd.memset(page[:], 0.0)
-        nc.gpsimd.memset(up_s[:].bitcast(I32), 0)
-        for page in page2:
-            nc.gpsimd.memset(page[:], 0.0)
+
+        page1 = [sbuf([P, T], F32, "page1_%d" % c) for c in range(TILES - 1)]
+        for page in page1:
+            nc.vector.memset(page[:], 0.0)
 
         x1_s = sbuf([P, J], U8, "x1_s")
         x2_s = sbuf([P, J], U8, "x2_s")
@@ -103,17 +88,20 @@ def tile_list_two_roads_one_layer_kernel(
         x2_w = [sbuf([P, J], U32, "x2_w%d" % z) for z in range(PASSES)]
         nc.vector.tensor_copy(x1_s[:], xq_s[:].indirect(list1[:]))
         nc.sync.dma_start(x1_s_hi[0:112, :].bitcast(I32), x1_s[4:116, :].bitcast(I32))
+        nc.vector.memset(low_s[:].bitcast(I32), 0)
+        for q in range(4):
+            nc.sync.dma_start(
+                low_s[32 * q : 32 * q + 8, :].bitcast(I32), low_scales[:, 4 * q : 4 * q + 4, :].bitcast(I32)
+            )
         nc.vector.tensor_copy(x2_s[:], xq_s[:].indirect(list2[:]))
+        low_w = sbuf([P, PASSES * R], I32, "low_w", tag="xq_s")
+        nc.scalar.dma_start(
+            low_w[:].rearrange("p (z c) -> p z c", z=PASSES),
+            low_words.rearrange("z p r i -> p z (r i)").bitcast(I32),
+        )
         for x_w, entries in ((x1_w, list1), (x2_w, list2)):
             for z in range(PASSES):
                 nc.vector.tensor_copy(x_w[z][:], xq_w[:, T * z : T * (z + 1)].bitcast(U32).indirect(entries[:]))
-
-        up_w = sbuf([P, 2 * N], U8, "up_w", tag="xq_s")
-        nc.sync.dma_start(up_w[:].bitcast(I32), up_words[0].bitcast(I32))
-        for q in range(4):
-            nc.sync.dma_start(
-                up_s[32 * q : 32 * q + 4, :].bitcast(I32), up_scales[0, 4 * q : 4 * q + 4, :].bitcast(I32)
-            )
 
         ga_bank = bank(0, "ga_bank")
         for m in range(4):
@@ -150,8 +138,8 @@ def tile_list_two_roads_one_layer_kernel(
             place_first(c, first_road(c), 0, J, None)
 
         u_banks = [bank(2 + c, "u_bank%d" % c) for c in range(TILES)]
-        for z in range(PASSES):
-            for c in range(TILES):
+        for c in range(TILES):
+            for z in range(PASSES):
                 nc.tensor.matmul_mx(
                     out=u_banks[c][:],
                     lhsT=x2_w[z][:, P * c : P * (c + 1)].bitcast(FP8X4),
@@ -161,6 +149,14 @@ def tile_list_two_roads_one_layer_kernel(
                     start=(z == 0),
                     stop=(z == PASSES - 1),
                 )
+
+        page1.append(sbuf([P, T], F32, "page1_3", tag="xq_w"))
+        page2 = [sbuf([P, T], F32, "page2_%d" % c, tag=("x2_w0", "x2_w1", "xq_s")[c]) for c in range(TILES - 1)]
+        up_s = sbuf([P, N], U8, "up_s", tag="x2_s")
+        nc.gpsimd.memset(page1[3][:], 0.0)
+        nc.gpsimd.memset(up_s[:].bitcast(I32), 0)
+        for page in page2:
+            nc.gpsimd.memset(page[:], 0.0)
 
         v_bf = sbuf([P, 4 * J], BF16, "v_bf")
         for c in range(TILES):
@@ -184,12 +180,22 @@ def tile_list_two_roads_one_layer_kernel(
                 v_bank[:].rearrange("p (t i) -> p i t", t=4),
             )
 
+        page2.append(sbuf([P, T], F32, "page2_3", tag="u_abs0"))
+        nc.gpsimd.memset(page2[3][:], 0.0)
+
         v_w = sbuf([P, J], U32, "v_w")
         v_s = sbuf([P, J], U8, "v_s")
         nc.vector.quantize_mx(out=v_w[:].bitcast(FP8X4), scales=v_s[:], in_=v_bf[:])
 
         p_last = first_road(TILES - 1)
         place_first(TILES - 1, p_last, 0, SPLIT, "u_half%d" % (TILES - 1))
+
+        up_w = sbuf([P, 2 * N], U8, "up_w", tag="wa_w")
+        nc.sync.dma_start(up_w[:].bitcast(I32), up_words[0].bitcast(I32))
+        for q in range(4):
+            nc.sync.dma_start(
+                up_s[32 * q : 32 * q + 4, :].bitcast(I32), up_scales[0, 4 * q : 4 * q + 4, :].bitcast(I32)
+            )
 
         q_sb = []
         for c in range(TILES):
@@ -206,37 +212,42 @@ def tile_list_two_roads_one_layer_kernel(
             q_sb.append(sbuf([P, J], F32, "q_sb%d" % c))
             nc.scalar.copy(q_sb[c][:], acc[:])
 
+        def add_transposed(sum_bank, page, h, first):
+            for j in range(4):
+                nc.tensor.matmul(
+                    sum_bank[:, P * j : P * (j + 1)],
+                    lhsT=page[:, BANK * h + P * j : BANK * h + P * (j + 1)],
+                    rhs=ident[:],
+                    is_transpose=True,
+                    start=(first and j == 0),
+                    stop=(not first and j == 3),
+                )
+
         for c in range(TILES):
             nc.vector.tensor_copy(page2[c][:].indirect(list2[:]), q_sb[c][:])
 
         for c in range(TILES - 1):
             if c == TILES - 2:
                 place_first(TILES - 1, p_last, SPLIT, J, "y_t%d_1" % (c - 1))
-            pages = (page1[c], page2[c])
+            y = sbuf([P, T], F32, "y%d" % c)
             for h in range(2):
                 cols = slice(BANK * h, BANK * (h + 1))
-                y = sbuf([P, BANK], F32, "y%d_%d" % (c, h))
                 sum_bank = bank(h, "sum_bank%d_%d" % (c, h))
-                for s in range(2):
-                    for j in range(4):
-                        nc.tensor.matmul(
-                            sum_bank[:, P * j : P * (j + 1)],
-                            lhsT=pages[s][:, BANK * h + P * j : BANK * h + P * (j + 1)],
-                            rhs=ident[:],
-                            is_transpose=True,
-                            start=(s == 0 and j == 0),
-                            stop=(s == 1 and j == 3),
-                        )
+                add_transposed(sum_bank, page1[c], h, True)
+                add_transposed(sum_bank, page2[c], h, False)
                 y_t = sbuf([P, BANK], F32, "y_t%d_%d" % (c, h))
                 nc.scalar.copy(y_t[:], sum_bank[:])
                 back_bank = bank(2 + h, "back_bank%d_%d" % (c, h))
                 for j in range(4):
                     nc.tensor.transpose(back_bank[:, P * j : P * (j + 1)], y_t[:, P * j : P * (j + 1)], ident[:])
-                nc.scalar.copy(y[:], back_bank[:])
-                nc.scalar.dma_start(out[P * c : P * (c + 1), cols], y[:])
+                nc.scalar.copy(y[:, cols], back_bank[:])
+                if c == TILES - 2:
+                    nc.scalar.dma_start(out[P * c : P * (c + 1), cols], y[:, cols])
+            if c < TILES - 2:
+                nc.scalar.dma_start(out[P * c : P * (c + 1), :], y[:])
 
         c = TILES - 1
-        for t0, t1, queue in ((0, 512, nc.sync), (512, 768, nc.sync), (768, 1024, nc.sync)):
+        for t0, t1 in ((0, 512), (512, 768), (768, 1024)):
             y = sbuf([P, t1 - t0], F32, "y_last%d" % t0)
             nc.vector.tensor_tensor(y[:], page1[c][:, t0:t1], page2[c][:, t0:t1], ALU.add)
-            queue.dma_start(out[P * c : P * (c + 1), t0:t1], y[:])
+            nc.sync.dma_start(out[P * c : P * (c + 1), t0:t1], y[:])

@@ -50,20 +50,20 @@ def tile_list_two_roads_one_layer_kernel(
         for plane in (wa_s, x1_s_hi):
             nc.vector.memset(plane[:].bitcast(I32), 0)
 
-        xq_w = sbuf([P, PASSES * T], I32, "xq_w")
+        xq_w = [sbuf([P, T], I32, "xq_w%d" % z) for z in range(PASSES)]
+        low_w = sbuf([P, PASSES * R], I32, "low_w")
         wa_w = sbuf([P, PASSES * 2 * N], U8, "wa_w")
         ga_col = sbuf([P, 4], F32, "ga_col")
 
         nc.sync.dma_start(list1[:], offs)
-        nc.sync.dma_start(list2[:], offs2)
+        nc.sync.dma_start(ga_col[:], ga.rearrange("o (p m) -> (o p) m", m=4))
         for q in range(4):
             nc.sync.dma_start(
                 xq_s[32 * q : 32 * q + 8, :].bitcast(I32), xq_scales[:, 4 * q : 4 * q + 4, :].bitcast(I32)
             )
-        nc.sync.dma_start(
-            xq_w[:].rearrange("p (z t) -> p z t", z=PASSES),
-            xq_words.rearrange("z p t i -> p z (t i)").bitcast(I32),
-        )
+        for z in range(PASSES):
+            nc.sync.dma_start(xq_w[z][:], xq_words[z].rearrange("p t i -> p (t i)").bitcast(I32))
+        nc.sync.dma_start(list2[:], offs2)
         nc.sync.dma_start(
             wa_w[:].bitcast(I32).rearrange("p (z c) -> p z c", z=PASSES),
             wa_words.bitcast(I32).rearrange("z p c -> p z c"),
@@ -73,7 +73,10 @@ def tile_list_two_roads_one_layer_kernel(
                 wa_s[32 * q : 32 * q + 4, :].bitcast(I32).rearrange("p (z c) -> p z c", z=PASSES),
                 wa_scales[:, 4 * q : 4 * q + 4, :].bitcast(I32).rearrange("z r c -> r z c"),
             )
-        nc.sync.dma_start(ga_col[:], ga.rearrange("o (p m) -> (o p) m", m=4))
+        nc.sync.dma_start(
+            low_w[:].rearrange("p (z c) -> p z c", z=PASSES),
+            low_words.rearrange("z p r i -> p z (r i)").bitcast(I32),
+        )
         ident = sbuf([P, P], F32, "ident")
         make_identity(nc, ident[:])
 
@@ -93,15 +96,11 @@ def tile_list_two_roads_one_layer_kernel(
             nc.sync.dma_start(
                 low_s[32 * q : 32 * q + 8, :].bitcast(I32), low_scales[:, 4 * q : 4 * q + 4, :].bitcast(I32)
             )
+        for z in range(PASSES):
+            nc.vector.tensor_copy(x1_w[z][:], xq_w[z][:].bitcast(U32).indirect(list1[:]))
         nc.vector.tensor_copy(x2_s[:], xq_s[:].indirect(list2[:]))
-        low_w = sbuf([P, PASSES * R], I32, "low_w", tag="xq_s")
-        nc.scalar.dma_start(
-            low_w[:].rearrange("p (z c) -> p z c", z=PASSES),
-            low_words.rearrange("z p r i -> p z (r i)").bitcast(I32),
-        )
-        for x_w, entries in ((x1_w, list1), (x2_w, list2)):
-            for z in range(PASSES):
-                nc.vector.tensor_copy(x_w[z][:], xq_w[:, T * z : T * (z + 1)].bitcast(U32).indirect(entries[:]))
+        for z in range(PASSES):
+            nc.vector.tensor_copy(x2_w[z][:], xq_w[z][:].bitcast(U32).indirect(list2[:]))
 
         ga_bank = bank(0, "ga_bank")
         for m in range(4):
@@ -150,8 +149,8 @@ def tile_list_two_roads_one_layer_kernel(
                     stop=(z == PASSES - 1),
                 )
 
-        page1.append(sbuf([P, T], F32, "page1_3", tag="xq_w"))
-        page2 = [sbuf([P, T], F32, "page2_%d" % c, tag=("x2_w0", "x2_w1", "xq_s")[c]) for c in range(TILES - 1)]
+        page1.append(sbuf([P, T], F32, "page1_3", tag="xq_w1"))
+        page2 = [sbuf([P, T], F32, "page2_%d" % c, tag="x2_w%d" % c) for c in range(2)]
         up_s = sbuf([P, N], U8, "up_s", tag="x2_s")
         nc.gpsimd.memset(page1[3][:], 0.0)
         nc.gpsimd.memset(up_s[:].bitcast(I32), 0)
@@ -179,9 +178,6 @@ def tile_list_two_roads_one_layer_kernel(
                 v_bf[:, 4 * P * c : 4 * P * (c + 1)].rearrange("p (i t) -> p i t", t=4),
                 v_bank[:].rearrange("p (t i) -> p i t", t=4),
             )
-
-        page2.append(sbuf([P, T], F32, "page2_3", tag="u_abs0"))
-        nc.gpsimd.memset(page2[3][:], 0.0)
 
         v_w = sbuf([P, J], U32, "v_w")
         v_s = sbuf([P, J], U8, "v_s")
@@ -223,18 +219,17 @@ def tile_list_two_roads_one_layer_kernel(
                     stop=(not first and j == 3),
                 )
 
-        for c in range(TILES):
-            nc.vector.tensor_copy(page2[c][:].indirect(list2[:]), q_sb[c][:])
-
         for c in range(TILES - 1):
+            nc.vector.tensor_copy(page2[c % 2][:].indirect(list2[:]), q_sb[c][:])
             if c == TILES - 2:
+                nc.vector.tensor_copy(page2[(c + 1) % 2][:].indirect(list2[:]), q_sb[c + 1][:])
                 place_first(TILES - 1, p_last, SPLIT, J, "y_t%d_1" % (c - 1))
             y = sbuf([P, T], F32, "y%d" % c)
             for h in range(2):
                 cols = slice(BANK * h, BANK * (h + 1))
                 sum_bank = bank(h, "sum_bank%d_%d" % (c, h))
                 add_transposed(sum_bank, page1[c], h, True)
-                add_transposed(sum_bank, page2[c], h, False)
+                add_transposed(sum_bank, page2[c % 2], h, False)
                 y_t = sbuf([P, BANK], F32, "y_t%d_%d" % (c, h))
                 nc.scalar.copy(y_t[:], sum_bank[:])
                 back_bank = bank(2 + h, "back_bank%d_%d" % (c, h))
@@ -249,5 +244,5 @@ def tile_list_two_roads_one_layer_kernel(
         c = TILES - 1
         for t0, t1 in ((0, 512), (512, 768), (768, 1024)):
             y = sbuf([P, t1 - t0], F32, "y_last%d" % t0)
-            nc.vector.tensor_tensor(y[:], page1[c][:, t0:t1], page2[c][:, t0:t1], ALU.add)
+            nc.vector.tensor_tensor(y[:], page1[c][:, t0:t1], page2[c % 2][:, t0:t1], ALU.add)
             nc.sync.dma_start(out[P * c : P * (c + 1), t0:t1], y[:])

from contextlib import ExitStack

import concourse.mybir as mybir
from concourse.masks import make_identity

K, T, J, N, R = 1024, 1024, 512, 512, 512
FLOPS = 2 * K * N * J + 2 * K * R * J + 2 * R * N * J

F32 = mybir.dt.float32
BF16 = mybir.dt.bfloat16
I32 = mybir.dt.int32
U32 = mybir.dt.uint32
U16 = mybir.dt.uint16
U8 = mybir.dt.uint8
FP8X4 = mybir.dt.float8_e4m3fn_x4
FP4X4 = mybir.dt.float4_e2m1fn_x4
ACT = mybir.ActivationFunctionType
ALU = mybir.AluOpType

P = 128
PASSES = K // 512
TILES = 4
BANK = 512
SPLIT = 320


def tile_list_two_roads_one_layer_kernel(
    tc, xq_words, xq_scales, wa_words, wa_scales, low_words, low_scales, up_words, up_scales, ga, offs, offs2, out
):
    nc = tc.nc
    with ExitStack() as ctx:
        lists = ctx.enter_context(tc.tile_pool(name="lists", bufs=1))
        sb = ctx.enter_context(tc.tile_pool(name="sb", bufs=1))
        psum = ctx.enter_context(tc.psum_pool(name="psum", bufs=1))

        def sbuf(shape, dtype, name, tag=None):
            return sb.tile(shape, dtype, name=name, tag=tag or name, align_bytes=64)

        def bank(b, name):
            return psum.tile([P, BANK], F32, name=name, tag="bank%d" % b)

        list1 = lists.tile([P, J // 16], U16, name="list1")
        list2 = lists.tile([P, J // 16], U16, name="list2")

        xq_s = sbuf([P, T], U8, "xq_s")
        wa_s = sbuf([P, PASSES * N], U8, "wa_s")
        low_s = sbuf([P, R], U8, "low_s")
        x1_s_hi = sbuf([P, J], U8, "x1_s_hi")
        nc.gpsimd.memset(xq_s[:].bitcast(I32), 0)
        for plane in (wa_s, x1_s_hi):
            nc.vector.memset(plane[:].bitcast(I32), 0)

        xq_w = [sbuf([P, T], I32, "xq_w%d" % z) for z in range(PASSES)]
        low_w = sbuf([P, PASSES * R], I32, "low_w")
        wa_w = sbuf([P, PASSES * 2 * N], U8, "wa_w")
        ga_col = sbuf([P, 4], F32, "ga_col")

        nc.sync.dma_start(list1[:], offs)
        nc.sync.dma_start(ga_col[:], ga.rearrange("o (p m) -> (o p) m", m=4))
        for q in range(4):
            nc.sync.dma_start(
                xq_s[32 * q : 32 * q + 8, :].bitcast(I32), xq_scales[:, 4 * q : 4 * q + 4, :].bitcast(I32)
            )
        for z in range(PASSES):
            nc.sync.dma_start(xq_w[z][:], xq_words[z].rearrange("p t i -> p (t i)").bitcast(I32))
        nc.sync.dma_start(list2[:], offs2)
        nc.sync.dma_start(
            wa_w[:].bitcast(I32).rearrange("p (z c) -> p z c", z=PASSES),
            wa_words.bitcast(I32).rearrange("z p c -> p z c"),
        )
        for q in range(4):
            nc.sync.dma_start(
                wa_s[32 * q : 32 * q + 4, :].bitcast(I32).rearrange("p (z c) -> p z c", z=PASSES),
                wa_scales[:, 4 * q : 4 * q + 4, :].bitcast(I32).rearrange("z r c -> r z c"),
            )
        nc.sync.dma_start(
            low_w[:].rearrange("p (z c) -> p z c", z=PASSES),
            low_words.rearrange("z p r i -> p z (r i)").bitcast(I32),
        )
        ident = sbuf([P, P], F32, "ident")
        make_identity(nc, ident[:])


        page1 = [sbuf([P, T], F32, "page1_%d" % c) for c in range(TILES - 1)]
        for page in page1:
            nc.vector.memset(page[:], 0.0)

        x1_s = sbuf([P, J], U8, "x1_s")
        x2_s = sbuf([P, J], U8, "x2_s")
        x1_w = [sbuf([P, J], U32, "x1_w%d" % z) for z in range(PASSES)]
        x2_w = [sbuf([P, J], U32, "x2_w%d" % z) for z in range(PASSES)]
        nc.vector.tensor_copy(x1_s[:], xq_s[:].indirect(list1[:]))
        nc.sync.dma_start(x1_s_hi[0:112, :].bitcast(I32), x1_s[4:116, :].bitcast(I32))
        nc.vector.memset(low_s[:].bitcast(I32), 0)
        for q in range(4):
            nc.sync.dma_start(
                low_s[32 * q : 32 * q + 8, :].bitcast(I32), low_scales[:, 4 * q : 4 * q + 4, :].bitcast(I32)
            )
        for z in range(PASSES):
            nc.vector.tensor_copy(x1_w[z][:], xq_w[z][:].bitcast(U32).indirect(list1[:]))
        nc.vector.tensor_copy(x2_s[:], xq_s[:].indirect(list2[:]))
        for z in range(PASSES):
            nc.vector.tensor_copy(x2_w[z][:], xq_w[z][:].bitcast(U32).indirect(list2[:]))

        ga_bank = bank(0, "ga_bank")
        for m in range(4):
            nc.tensor.transpose(ga_bank[:, P * m : P * (m + 1)], ga_col[:, m : m + 1].to_broadcast([P, P]), ident[:])
        ga_all = sbuf([P, J], F32, "ga_all")
        nc.scalar.activation(
            ga_all[:].rearrange("p (j m) -> p j m", m=4), ga_bank[:].rearrange("p (m j) -> p j m", m=4), ACT.Copy
        )

        x1_planes = (x1_s, x1_s_hi)

        def first_road(c):
            acc = bank(4 + c, "p_bank%d" % c)
            for z in range(PASSES):
                nc.tensor.matmul_mx(
                    out=acc[:],
                    lhsT=wa_w[:, 2 * (N * z + P * c) : 2 * (N * z + P * (c + 1))].bitcast(FP4X4),
                    lhsT_scale=wa_s[:, N * z + P * c : N * z + P * (c + 1)],
                    rhs=x1_w[z][:].bitcast(FP8X4),
                    rhs_scale=x1_planes[z][:],
                    start=(z == 0),
                    stop=(z == PASSES - 1),
                )
            return acc

        def place_first(c, acc, j0, j1, tag):
            p_sb = sbuf([P, J], F32, "p_sb%d_%d" % (c, j0), tag=tag)
            nc.scalar.copy(p_sb[:, j0:j1], acc[:, j0:j1])
            nc.vector.tensor_tensor(
                page1[c][:].indirect(list1[:, j0 // 16 : j1 // 16]), p_sb[:, j0:j1], ga_all[:, j0:j1], ALU.mult
            )

        for c in range(TILES - 1):
            place_first(c, first_road(c), 0, J, None)

        u_banks = [bank(2 + c, "u_bank%d" % c) for c in range(TILES)]
        for c in range(TILES):
            for z in range(PASSES):
                nc.tensor.matmul_mx(
                    out=u_banks[c][:],
                    lhsT=x2_w[z][:, P * c : P * (c + 1)].bitcast(FP8X4),
                    lhsT_scale=x2_s[4 * z : P, P * c : P * (c + 1)],
                    rhs=low_w[:, R * z : R * (z + 1)].bitcast(FP8X4),
                    rhs_scale=low_s[4 * z : P, :],
                    start=(z == 0),
                    stop=(z == PASSES - 1),
                )

        page1.append(sbuf([P, T], F32, "page1_3", tag="xq_w1"))
        page2 = [sbuf([P, T], F32, "page2_%d" % c, tag="x2_w%d" % c) for c in range(2)]
        up_s = sbuf([P, N], U8, "up_s", tag="x2_s")
        nc.gpsimd.memset(page1[3][:], 0.0)
        nc.gpsimd.memset(up_s[:].bitcast(I32), 0)
        for page in page2:
            nc.gpsimd.memset(page[:], 0.0)

        v_bf = sbuf([P, 4 * J], BF16, "v_bf")
        for c in range(TILES):
            u_dealt = u_banks[c][:].rearrange("p (q t) -> p t q", t=4)
            terms = [sbuf([P, R], F32, "u_abs%d" % c), sbuf([P, R], F32, "u_half%d" % c)]
            nc.scalar.activation(terms[0][:].rearrange("p (t q) -> p t q", t=4), u_dealt, ACT.Abs)
            nc.scalar.activation(terms[1][:].rearrange("p (t q) -> p t q", t=4), u_dealt, ACT.Copy, scale=-0.5)
            v_bank = bank(c % 2, "v_bank%d" % c)
            for s in range(2):
                for t in range(4):
                    nc.tensor.matmul(
                        v_bank[:, P * t : P * (t + 1)],
                        lhsT=terms[s][:, P * t : P * (t + 1)],
                        rhs=ident[:],
                        is_transpose=True,
                        start=(s == 0 and t == 0),
                        stop=(s == 1 and t == 3),
                    )
            nc.scalar.copy(
                v_bf[:, 4 * P * c : 4 * P * (c + 1)].rearrange("p (i t) -> p i t", t=4),
                v_bank[:].rearrange("p (t i) -> p i t", t=4),
            )

        v_w = sbuf([P, J], U32, "v_w")
        v_s = sbuf([P, J], U8, "v_s")
        nc.vector.quantize_mx(out=v_w[:].bitcast(FP8X4), scales=v_s[:], in_=v_bf[:])

        p_last = first_road(TILES - 1)
        place_first(TILES - 1, p_last, 0, SPLIT, "u_half%d" % (TILES - 1))

        up_w = sbuf([P, 2 * N], U8, "up_w", tag="wa_w")
        nc.sync.dma_start(up_w[:].bitcast(I32), up_words[0].bitcast(I32))
        for q in range(4):
            nc.sync.dma_start(
                up_s[32 * q : 32 * q + 4, :].bitcast(I32), up_scales[0, 4 * q : 4 * q + 4, :].bitcast(I32)
            )

        q_sb = []
        for c in range(TILES):
            acc = bank((6, 4, 5, 2)[c], "q_bank%d" % c)
            nc.tensor.matmul_mx(
                out=acc[:],
                lhsT=up_w[:, 2 * P * c : 2 * P * (c + 1)].bitcast(FP4X4),
                lhsT_scale=up_s[:, P * c : P * (c + 1)],
                rhs=v_w[:].bitcast(FP8X4),
                rhs_scale=v_s[:],
                start=True,
                stop=True,
            )
            q_sb.append(sbuf([P, J], F32, "q_sb%d" % c))
            nc.scalar.copy(q_sb[c][:], acc[:])

        def add_transposed(sum_bank, page, h, first):
            for j in range(4):
                nc.tensor.matmul(
                    sum_bank[:, P * j : P * (j + 1)],
                    lhsT=page[:, BANK * h + P * j : BANK * h + P * (j + 1)],
                    rhs=ident[:],
                    is_transpose=True,
                    start=(first and j == 0),
                    stop=(not first and j == 3),
                )

        for c in range(TILES - 1):
            nc.vector.tensor_copy(page2[c % 2][:].indirect(list2[:]), q_sb[c][:])
            if c == TILES - 2:
                nc.vector.tensor_copy(page2[(c + 1) % 2][:].indirect(list2[:]), q_sb[c + 1][:])
                place_first(TILES - 1, p_last, SPLIT, J, "y_t%d_1" % (c - 1))
            y = sbuf([P, T], F32, "y%d" % c)
            for h in range(2):
                cols = slice(BANK * h, BANK * (h + 1))
                sum_bank = bank(h, "sum_bank%d_%d" % (c, h))
                add_transposed(sum_bank, page1[c], h, True)
                add_transposed(sum_bank, page2[c % 2], h, False)
                y_t = sbuf([P, BANK], F32, "y_t%d_%d" % (c, h))
                nc.scalar.copy(y_t[:], sum_bank[:])
                back_bank = bank(2 + h, "back_bank%d_%d" % (c, h))
                for j in range(4):
                    nc.tensor.transpose(back_bank[:, P * j : P * (j + 1)], y_t[:, P * j : P * (j + 1)], ident[:])
                nc.scalar.copy(y[:, cols], back_bank[:])
                if c == TILES - 2:
                    nc.scalar.dma_start(out[P * c : P * (c + 1), cols], y[:, cols])
            if c < TILES - 2:
                nc.scalar.dma_start(out[P * c : P * (c + 1), :], y[:])

        c = TILES - 1
        for t0, t1 in ((0, 512), (512, 768), (768, 1024)):
            y = sbuf([P, t1 - t0], F32, "y_last%d" % t0)
            nc.vector.tensor_tensor(y[:], page1[c][:, t0:t1], page2[c % 2][:, t0:t1], ALU.add)
            nc.sync.dma_start(out[P * c : P * (c + 1), t0:t1], y[:])
